import numpy as np, ml_dtypes
CORES = [50,106,114,52,108,116]
N = 6
import mx_ref
NC, G, D = 128, 2, 64
C = np.float32(0.041)
BF = ml_dtypes.bfloat16
def cut(t, i, w=512):
    return t[:, w * i:w * i + w]
def tile(rs):
    return np.stack(rs, axis=2).reshape(128, -1).astype(BF)
def layer(w, X):
    out = []
    for i in range(G):
        for t in range(len(X)):
            p = mx_ref.matmul(mx_ref.quantize(cut(w, len(X) * i + t)), X[t])
            z = p if t == 0 else z + p
        out.append(z)
    return out
def act(Z):
    return [np.maximum(s * z, 0) * C for z in Z for s in (1, -1)]
def setup_inputs(rng):
    def f(*shape):
        return mx_ref.flush((rng.standard_normal(shape, dtype=np.float32) * np.exp2(rng.integers(-2, 3, shape[:-1] + (1,)))).astype(BF))
    return {"x": f(N, 128, 4 * NC), "w1": f(N, 128, G * 512), "wt": f(N, 128, 3 * 512)}
def setup_inputs_blocks(rng):
    d = setup_inputs(rng)
    for k in ("x", "wt", "w1"): d[k] = mx_ref.spread(d[k], rng, 2)
    return d
def setup_inputs_wide(rng):
    d = setup_inputs(rng)
    for k in ("wt",): d[k] = mx_ref.flush((d[k].astype(np.float32) * np.exp2(rng.integers(-6, 7, (N, 1, 1))).astype(np.float32)).astype(BF))
    return d
def setup_inputs_zeros(rng):
    d = setup_inputs(rng); v = d["x"].reshape(N, 128, -1, 4).copy()
    v[np.broadcast_to((rng.random((N, 1, v.shape[2], 1)) < 0.33), v.shape)] = 0
    d["x"] = v.reshape(d["x"].shape)
    return d
def reference(x, w1, wt):
    h = [tile(act(layer(w1[j], [mx_ref.quantize(x[j])]))) for j in range(N)]
    y = np.zeros((N, 128, NC), np.float32)
    for r in range(N):
        e = np.concatenate([h[(r - 1) % N][:, 4 * (NC - D):], h[r], h[(r + 1) % N][:, :4 * D]], axis=1)
        for t in range(3):
            p = mx_ref.matmul(mx_ref.quantize(cut(wt[r], t)), mx_ref.quantize(e[:, 4 * D * t:4 * D * t + 4 * NC]))
            y[r] = p if t == 0 else y[r] + p
    return {"y": y}

from concourse.bass import DstId, RemoteDMATransfer
from concourse.mybir import dt, AluOpType, ActivationFunctionType

NC, D = 128, 64
C = 0.041

SCRATCH = {
    "xt": ("sbuf", [128, 512], "bfloat16"),
    "w1t": ("sbuf", [128, 1024], "bfloat16"),
    "wtt": ("sbuf", [128, 1536], "bfloat16"),
    "ht": ("sbuf", [128, 512], "bfloat16"),
    "xq": ("sbuf", [128, 128], "float8_e4m3fn_x4"),
    "xs": ("sbuf", [128, 128], "uint8"),
    "w1q": ("sbuf", [128, 256], "float8_e4m3fn_x4"),
    "w1s": ("sbuf", [128, 256], "uint8"),
    "wq": ("sbuf", [128, 384], "float8_e4m3fn_x4"),
    "ws": ("sbuf", [128, 384], "uint8"),
    "eq": ("sbuf", [128, 256], "float8_e4m3fn_x4"),
    "es": ("sbuf", [128, 256], "uint8"),
    "pq": ("sbuf", [128, 128], "float8_e4m3fn_x4"),
    "ps": ("sbuf", [128, 128], "uint8"),
    "ysb": ("sbuf", [128, 128], "float32"),
    "z0": ("psum", [128, 512], "float32"),
    "z1": ("psum", [128, 512], "float32"),
    "yp": ("psum", [128, 512], "float32"),
}
SEMAPHORES = ["lx", "lw", "lt", "ly", "qx", "q0", "q1", "z0", "z1", "r", "hq", "tq", "yd", "yc",
              "left", "right", "pcode", "pscale", "sent"]


def _bits(mask):
    return [1 << k for k in range(mask.bit_length()) if mask >> k & 1]


def rank_program(g, core, T, topo):
    rank = T.rank_of(core)
    if rank is None:
        return
    cores, n = T.cores, len(T.cores)
    S = T.sem

    edges = []
    for r in range(n):
        edges.append((r, (r + 1) % n, NC - D, 0, "left"))
        edges.append((r, (r - 1) % n, 0, NC + D, "right"))

    def via(e):
        a, b = cores[e[0]], cores[e[1]]
        if topo.may_write(a, b):
            return None
        return [q for q in range(n) if q not in e[:2] and topo.chip(cores[q]) == topo.chip(a)
                and topo.may_write(cores[q], b)][0]

    def part(engines, k, of):
        return sum(engines[k::of])

    def masks(es):
        src, of = es[0][0], len(es)
        return [part(_bits(topo.mask(src, dst)), k, of) for k, (_, dst) in enumerate(es)]

    def count(mask):
        return len(_bits(mask))

    def to(c):
        rid, pid, _ = topo.addr(c)
        return DstId(rid=rid, pnc=pid)

    def out_edges(q):
        own = [e for e in edges if e[0] == q and via(e) is None]
        passed = [e for e in edges if via(e) == q]
        return own, passed

    def edge_mask(e):
        q = via(e)
        own, passed = out_edges(e[0] if q is None else q)
        group = own if q is None else passed
        src = cores[e[0] if q is None else q]
        return masks([(src, cores[f[1]]) for f in group])[group.index(e)]

    def hop_mask(a, b):
        return part(_bits(topo.mask(a, b)), 0, 2)

    g.sync.dma_start(T.xt[:], T.x[:]).then_inc(S.lx, 16)
    g.scalar.dma_start(T.w1t[:], T.w1[:]).then_inc(S.lw, 16)
    g.sync.wait_ge(S.lx, 16)
    g.sync.dma_start(T.wtt[:], T.wt[:]).then_inc(S.lt, 16)
    g.sync.wait_ge(S.yc, 1)
    g.sync.dma_start(T.y[:], T.ysb[:]).then_inc(S.ly, 16)
    g.sync.wait_ge(S.ly, 16)

    v = g.vector
    v.wait_ge(S.lx, 16)
    v.quantize_mx(T.xq[:], T.xs[:], T.xt[:]).then_inc(S.qx, 1)
    v.wait_ge(S.lw, 16)
    v.quantize_mx(T.w1q[:, 0:128], T.w1s[:, 0:128], T.w1t[:, 0:512]).then_inc(S.q0, 1)
    v.quantize_mx(T.w1q[:, 128:256], T.w1s[:, 128:256], T.w1t[:, 512:1024]).then_inc(S.q1, 1)
    v.wait_ge(S.z1, 1)
    v.tensor_scalar(T.ht[:, 2:512:4], T.z1[:, 0:NC], 0.0, C, AluOpType.max, AluOpType.mult).then_inc(S.r, 1)
    v.tensor_scalar(T.ht[:, 3:512:4], T.z1[:, 0:NC], 0.0, -C, AluOpType.min, AluOpType.mult).then_inc(S.r, 1)
    v.wait_ge(S.r, 4)
    v.quantize_mx(T.eq[:, D:D + NC], T.es[:, D:D + NC], T.ht[:]).then_inc(S.hq, 1)
    v.wait_ge(S.lt, 16)
    v.quantize_mx(T.wq[:], T.ws[:], T.wtt[:]).then_inc(S.tq, 1)
    v.wait_ge(S.yd, 1)
    v.tensor_copy(T.ysb[:], T.yp[:, 0:NC]).then_inc(S.yc, 1)

    relu = ActivationFunctionType.Relu
    g.scalar.wait_ge(S.z0, 1)
    g.scalar.activation(T.ht[:, 0:512:4], T.z0[:, 0:NC], relu, scale=C).then_inc(S.r, 1)
    g.scalar.activation(T.ht[:, 1:512:4], T.z0[:, 0:NC], relu, scale=-C).then_inc(S.r, 1)

    t = g.tensor
    t.wait_ge(S.qx, 1)
    t.wait_ge(S.q0, 1)
    t.matmul_mx(T.z0[:, 0:NC], T.w1q[:, 0:128], T.w1s[:, 0:128], T.xq[:], T.xs[:], True, True).then_inc(S.z0, 1)
    t.wait_ge(S.q1, 1)
    t.matmul_mx(T.z1[:, 0:NC], T.w1q[:, 128:256], T.w1s[:, 128:256], T.xq[:], T.xs[:], True, True).then_inc(S.z1, 1)

    def tap(k, start, stop):
        return t.matmul_mx(T.yp[:, 0:NC], T.wq[:, 128 * k:128 * k + 128], T.ws[:, 128 * k:128 * k + 128],
                           T.eq[:, D * k:D * k + NC], T.es[:, D * k:D * k + NC], start, stop)

    t.wait_ge(S.hq, 1)
    t.wait_ge(S.tq, 1)
    tap(1, True, False)
    halos = sorted([e for e in edges if e[1] == rank], key=lambda e: (via(e) is not None, e[3]))
    for i, e in enumerate(halos):
        t.wait_ge(S[e[4]], 2 * count(edge_mask(e)))
        m = tap(e[3] // (NC - D) * 2 // 3 if e[3] else 0, False, i == 1)
    m.then_inc(S.yd, 1)

    sent = [0]

    def send(items, cq, cs, at):
        def call(code):
            ts = []
            for e, mk in items:
                c, d = at(e), e[3]
                if code:
                    src, dst = cq[:, c:c + D].bitcast(dt.uint8), T.eq[:, d:d + D].bitcast(dt.uint8)
                else:
                    src, dst = cs[:, c:c + D], T.es[:, d:d + D]
                ts.append(RemoteDMATransfer(dst_ids=[to(cores[e[1]])], dma_engine_mask=mk, remote_sem=S[e[4]],
                                            src=src, dst=dst))
                sent[0] += count(mk)
            g.remote_dma_fused(ts, local_sem=S.sent)
        return call

    own, passed = out_edges(rank)
    handed = [e for e in edges if e[0] == rank and via(e) is not None]
    g.wait_ge(S.hq, 1)
    if handed:
        a = min(e[2] for e in handed)
        b = max(e[2] for e in handed) + D
        q = cores[via(handed[0])]
        rid, pid, _ = topo.addr(q)
        mk = hop_mask(core, q)
        g.remote_dma(T.pq[:, a:b].bitcast(dt.uint8), T.eq[:, D + a:D + b].bitcast(dt.uint8), S.pcode, S.sent,
                     pid, rid, mk)
        g.remote_dma(T.ps[:, a:b], T.es[:, D + a:D + b], S.pscale, S.sent, pid, rid, mk)
        sent[0] += 2 * count(mk)
    if own:
        call = send([(e, edge_mask(e)) for e in own], T.eq, T.es, lambda e: D + e[2])
        call(True)
        call(False)
    if passed:
        k = count(hop_mask(cores[passed[0][0]], core))
        call = send([(e, edge_mask(e)) for e in passed], T.pq, T.ps, lambda e: e[2])
        g.wait_ge(S.pcode, k)
        call(True)
        g.wait_ge(S.pscale, k)
        call(False)
    g.wait_ge(S.sent, sent[0])
